import numpy as np
import ml_dtypes

BF16 = ml_dtypes.bfloat16


def bf(x):
    return np.asarray(x, np.float32).astype(BF16)


def f32(x):
    return np.asarray(x, np.float32)


def f64(x):
    return np.asarray(x).astype(np.float64)


def striped(idx):
    return np.concatenate([l.reshape(-1, 16).T for l in idx])


def rows(idx, k):
    return np.tile(np.repeat(idx, 16, axis=0), (k // (16 * 8), 1))


def look(tab, idx):
    return np.take_along_axis(f64(tab), rows(idx, len(tab)), axis=1)


K, S, V, N, M = 128, 2048, 1536, 1536, 128


def setup_inputs():
    return {"tab": f32(np.random.standard_normal((K, S))), "w": bf(np.random.standard_normal((K, M)) / np.sqrt(K)), "b": f32(0.5 * np.random.standard_normal((M, 1))), "offs": striped(np.random.randint(0, S, (8, N)))}


def reference(tab, w, b, offs):
    idx = np.stack([g.T.reshape(-1) for g in np.split(offs, 8)])
    t = look(tab, idx)
    x = np.minimum(np.maximum(t, -1.25), 1.0)
    y = f64(w).T @ x
    return np.maximum(y + f64(b), 0.0)

@@ -1,0 +1,44 @@
+import concourse.mybir as mybir
+
+F32, BF16, U16 = mybir.dt.float32, mybir.dt.bfloat16, mybir.dt.uint16
+ALU = mybir.AluOpType
+ACT = mybir.ActivationFunctionType
+
+ROWS, TABLE, ENTRIES, OUTPUTS = 128, 2048, 1536, 128
+CLAMP_LOW, CLAMP_HIGH = -1.25, 1.0
+GROUP = 16
+PIECE = 512
+PIECES = ENTRIES // PIECE
+
+FLOPS = 2 * ROWS * OUTPUTS * ENTRIES
+
+
+def tile_lookup_deq_clip_relu_kernel(tc, tab, w, b, offs, out):
+    nc = tc.nc
+    with (
+        tc.tile_pool(name="held", bufs=1) as held,
+        tc.tile_pool(name="work", bufs=PIECES) as work,
+        tc.psum_pool(name="psum", bufs=PIECES) as psum,
+    ):
+        offsets = held.tile([ROWS, ENTRIES // GROUP], U16, name="offsets")
+        table = held.tile([ROWS, TABLE], F32, name="table")
+        weights = held.tile([ROWS, OUTPUTS], BF16, name="weights")
+        bias = held.tile([OUTPUTS, 1], F32, name="bias")
+        nc.sync.dma_start(offsets[:], offs)
+        nc.sync.dma_start(table[:], tab)
+        nc.sync.dma_start(weights[:], w)
+        nc.sync.dma_start(bias[:], b)
+
+        for piece in range(PIECES):
+            piece_offsets = offsets[:, piece * PIECE // GROUP : (piece + 1) * PIECE // GROUP]
+            clamped = work.tile([ROWS, PIECE], F32, name="clamped")
+            nc.vector.tensor_scalar(
+                clamped[:], table[:].indirect(piece_offsets), CLAMP_LOW, CLAMP_HIGH, ALU.max, ALU.min
+            )
+            rounded = work.tile([ROWS, PIECE], BF16, name="rounded")
+            nc.scalar.copy(rounded[:], clamped[:])
+            product = psum.tile([OUTPUTS, PIECE], F32, name="product")
+            nc.tensor.matmul(product[:], weights[:], rounded[:], start=True, stop=True)
+            result = work.tile([OUTPUTS, PIECE], F32, name="result")
+            nc.scalar.activation(result[:], product[:], ACT.Relu, bias=bias[:])
+            nc.sync.dma_start(out[:, piece * PIECE : (piece + 1) * PIECE], result[:])

@@ -9,6 +9,8 @@ CLAMP_LOW, CLAMP_HIGH = -1.25, 1.0
 GROUP = 16
 PIECE = 512
 PIECES = ENTRIES // PIECE
+CHUNK = PIECE // 2
+CHUNKS = ENTRIES // CHUNK
 
 FLOPS = 2 * ROWS * OUTPUTS * ENTRIES
 
@@ -17,28 +19,39 @@ def tile_lookup_deq_clip_relu_kernel(tc, tab, w, b, offs, out):
     nc = tc.nc
     with (
         tc.tile_pool(name="held", bufs=1) as held,
-        tc.tile_pool(name="work", bufs=PIECES) as work,
-        tc.psum_pool(name="psum", bufs=PIECES) as psum,
+        tc.tile_pool(name="pieces", bufs=PIECES) as pieces,
+        tc.tile_pool(name="chunks", bufs=CHUNKS) as chunks,
+        tc.psum_pool(name="psum", bufs=CHUNKS) as psum,
     ):
         offsets = held.tile([ROWS, ENTRIES // GROUP], U16, name="offsets")
         table = held.tile([ROWS, TABLE], F32, name="table")
         weights = held.tile([ROWS, OUTPUTS], BF16, name="weights")
         bias = held.tile([OUTPUTS, 1], F32, name="bias")
         nc.sync.dma_start(offsets[:], offs)
-        nc.sync.dma_start(table[:], tab)
-        nc.sync.dma_start(weights[:], w)
-        nc.sync.dma_start(bias[:], b)
+        nc.scalar.dma_start(table[:], tab)
+        nc.scalar.dma_start(weights[:], w)
+        nc.scalar.dma_start(bias[:], b)
 
+        clamped = []
         for piece in range(PIECES):
             piece_offsets = offsets[:, piece * PIECE // GROUP : (piece + 1) * PIECE // GROUP]
-            clamped = work.tile([ROWS, PIECE], F32, name="clamped")
+            picked = pieces.tile([ROWS, PIECE], F32, name="picked")
             nc.vector.tensor_scalar(
-                clamped[:], table[:].indirect(piece_offsets), CLAMP_LOW, CLAMP_HIGH, ALU.max, ALU.min
+                picked[:], table[:].indirect(piece_offsets), CLAMP_LOW, CLAMP_HIGH, ALU.max, ALU.min
             )
-            rounded = work.tile([ROWS, PIECE], BF16, name="rounded")
-            nc.scalar.copy(rounded[:], clamped[:])
-            product = psum.tile([OUTPUTS, PIECE], F32, name="product")
+            clamped += [picked[:, :CHUNK], picked[:, CHUNK:]]
+
+        for chunk in range(CHUNKS):
+            rounded = chunks.tile([ROWS, CHUNK], BF16, name="rounded")
+            if chunk * CHUNK >= ENTRIES - PIECE:
+                nc.vector.tensor_copy(rounded[:], clamped[chunk])
+            else:
+                nc.scalar.copy(rounded[:], clamped[chunk])
+            product = psum.tile([OUTPUTS, CHUNK], F32, name="product")
             nc.tensor.matmul(product[:], weights[:], rounded[:], start=True, stop=True)
-            result = work.tile([OUTPUTS, PIECE], F32, name="result")
-            nc.scalar.activation(result[:], product[:], ACT.Relu, bias=bias[:])
-            nc.sync.dma_start(out[:, piece * PIECE : (piece + 1) * PIECE], result[:])
+            result = chunks.tile([OUTPUTS, CHUNK], F32, name="result")
+            if chunk == CHUNKS - 1:
+                nc.vector.tensor_scalar(result[:], product[:], bias[:], 0.0, ALU.add, ALU.max)
+            else:
+                nc.scalar.activation(result[:], product[:], ACT.Relu, bias=bias[:])
+            nc.sync.dma_start(out[:, chunk * CHUNK : (chunk + 1) * CHUNK], result[:])

@@ -28,9 +28,9 @@ def tile_lookup_deq_clip_relu_kernel(tc, tab, w, b, offs, out):
         weights = held.tile([ROWS, OUTPUTS], BF16, name="weights")
         bias = held.tile([OUTPUTS, 1], F32, name="bias")
         nc.sync.dma_start(offsets[:], offs)
-        nc.scalar.dma_start(table[:], tab)
-        nc.scalar.dma_start(weights[:], w)
-        nc.scalar.dma_start(bias[:], b)
+        nc.sync.dma_start(table[:], tab)
+        nc.sync.dma_start(weights[:], w)
+        nc.sync.dma_start(bias[:], b)
 
         clamped = []
         for piece in range(PIECES):

@@ -11,6 +11,8 @@ PIECE = 512
 PIECES = ENTRIES // PIECE
 CHUNK = PIECE // 2
 CHUNKS = ENTRIES // CHUNK
+WARMUP_COLUMNS = 512
+WARMUP_MATMULS = 16
 
 FLOPS = 2 * ROWS * OUTPUTS * ENTRIES
 
@@ -22,6 +24,7 @@ def tile_lookup_deq_clip_relu_kernel(tc, tab, w, b, offs, out):
         tc.tile_pool(name="pieces", bufs=PIECES) as pieces,
         tc.tile_pool(name="chunks", bufs=CHUNKS) as chunks,
         tc.psum_pool(name="psum", bufs=CHUNKS) as psum,
+        tc.psum_pool(name="spare", bufs=1) as spare,
     ):
         offsets = held.tile([ROWS, ENTRIES // GROUP], U16, name="offsets")
         table = held.tile([ROWS, TABLE], F32, name="table")
@@ -31,6 +34,14 @@ def tile_lookup_deq_clip_relu_kernel(tc, tab, w, b, offs, out):
         nc.sync.dma_start(table[:], tab)
         nc.sync.dma_start(weights[:], w)
         nc.sync.dma_start(bias[:], b)
+
+        zeros = held.tile([ROWS, WARMUP_COLUMNS], BF16, name="zeros")
+        nc.vector.memset(zeros[:], 0.0)
+        unused = spare.tile([OUTPUTS, WARMUP_COLUMNS], F32, name="unused")
+        for step in range(WARMUP_MATMULS):
+            nc.tensor.matmul(
+                unused[:], zeros[:, :OUTPUTS], zeros[:], start=step == 0, stop=step == WARMUP_MATMULS - 1
+            )
 
         clamped = []
         for piece in range(PIECES):

@@ -11,8 +11,9 @@ PIECE = 512
 PIECES = ENTRIES // PIECE
 CHUNK = PIECE // 2
 CHUNKS = ENTRIES // CHUNK
-WARMUP_COLUMNS = 512
-WARMUP_MATMULS = 16
+EARLY_CHUNKS = (ENTRIES - PIECE) // CHUNK
+HALF = CHUNK // 2
+PRODUCTS = EARLY_CHUNKS + PIECE // HALF
 
 FLOPS = 2 * ROWS * OUTPUTS * ENTRIES
 
@@ -22,9 +23,8 @@ def tile_lookup_deq_clip_relu_kernel(tc, tab, w, b, offs, out):
     with (
         tc.tile_pool(name="held", bufs=1) as held,
         tc.tile_pool(name="pieces", bufs=PIECES) as pieces,
-        tc.tile_pool(name="chunks", bufs=CHUNKS) as chunks,
-        tc.psum_pool(name="psum", bufs=CHUNKS) as psum,
-        tc.psum_pool(name="spare", bufs=1) as spare,
+        tc.tile_pool(name="chunks", bufs=PRODUCTS) as chunks,
+        tc.psum_pool(name="psum", bufs=PRODUCTS) as psum,
     ):
         offsets = held.tile([ROWS, ENTRIES // GROUP], U16, name="offsets")
         table = held.tile([ROWS, TABLE], F32, name="table")
@@ -35,14 +35,6 @@ def tile_lookup_deq_clip_relu_kernel(tc, tab, w, b, offs, out):
         nc.sync.dma_start(weights[:], w)
         nc.sync.dma_start(bias[:], b)
 
-        zeros = held.tile([ROWS, WARMUP_COLUMNS], BF16, name="zeros")
-        nc.vector.memset(zeros[:], 0.0)
-        unused = spare.tile([OUTPUTS, WARMUP_COLUMNS], F32, name="unused")
-        for step in range(WARMUP_MATMULS):
-            nc.tensor.matmul(
-                unused[:], zeros[:, :OUTPUTS], zeros[:], start=step == 0, stop=step == WARMUP_MATMULS - 1
-            )
-
         clamped = []
         for piece in range(PIECES):
             piece_offsets = offsets[:, piece * PIECE // GROUP : (piece + 1) * PIECE // GROUP]
@@ -52,17 +44,30 @@ def tile_lookup_deq_clip_relu_kernel(tc, tab, w, b, offs, out):
             )
             clamped += [picked[:, :CHUNK], picked[:, CHUNK:]]
 
-        for chunk in range(CHUNKS):
-            rounded = chunks.tile([ROWS, CHUNK], BF16, name="rounded")
-            if chunk * CHUNK >= ENTRIES - PIECE:
-                nc.vector.tensor_copy(rounded[:], clamped[chunk])
-            else:
-                nc.scalar.copy(rounded[:], clamped[chunk])
-            product = psum.tile([OUTPUTS, CHUNK], F32, name="product")
+        def multiply(values, round_to_bf16):
+            columns = values.shape[1]
+            rounded = chunks.tile([ROWS, columns], BF16, name="rounded")
+            round_to_bf16(rounded[:], values)
+            product = psum.tile([OUTPUTS, columns], F32, name="product")
             nc.tensor.matmul(product[:], weights[:], rounded[:], start=True, stop=True)
-            result = chunks.tile([OUTPUTS, CHUNK], F32, name="result")
-            if chunk == CHUNKS - 1:
-                nc.vector.tensor_scalar(result[:], product[:], bias[:], 0.0, ALU.add, ALU.max)
+            return product
+
+        products = []
+        for chunk in range(CHUNKS):
+            if chunk < EARLY_CHUNKS:
+                products.append([multiply(clamped[chunk], nc.scalar.copy)])
             else:
-                nc.scalar.activation(result[:], product[:], ACT.Relu, bias=bias[:])
+                products.append([
+                    multiply(clamped[chunk][:, :HALF], nc.vector.tensor_copy),
+                    multiply(clamped[chunk][:, HALF:], nc.vector.tensor_copy),
+                ])
+
+        for chunk in range(CHUNKS):
+            result = chunks.tile([OUTPUTS, CHUNK], F32, name="result")
+            if chunk < EARLY_CHUNKS:
+                nc.scalar.activation(result[:], products[chunk][0][:], ACT.Relu, bias=bias[:])
+            else:
+                left, right = products[chunk]
+                nc.scalar.activation(result[:, :HALF], left[:], ACT.Relu, bias=bias[:])
+                nc.vector.tensor_scalar(result[:, HALF:], right[:], bias[:], 0.0, ALU.add, ALU.max)
             nc.sync.dma_start(out[:, chunk * CHUNK : (chunk + 1) * CHUNK], result[:])

import concourse.mybir as mybir

F32, BF16, U16 = mybir.dt.float32, mybir.dt.bfloat16, mybir.dt.uint16
ALU = mybir.AluOpType
ACT = mybir.ActivationFunctionType

ROWS, TABLE, ENTRIES, OUTPUTS = 128, 2048, 1536, 128
CLAMP_LOW, CLAMP_HIGH = -1.25, 1.0
GROUP = 16
PIECE = 512
PIECES = ENTRIES // PIECE
CHUNK = PIECE // 2
CHUNKS = ENTRIES // CHUNK
EARLY_CHUNKS = (ENTRIES - PIECE) // CHUNK
HALF = CHUNK // 2
PRODUCTS = EARLY_CHUNKS + PIECE // HALF

FLOPS = 2 * ROWS * OUTPUTS * ENTRIES


def tile_lookup_deq_clip_relu_kernel(tc, tab, w, b, offs, out):
    nc = tc.nc
    with (
        tc.tile_pool(name="held", bufs=1) as held,
        tc.tile_pool(name="pieces", bufs=PIECES) as pieces,
        tc.tile_pool(name="chunks", bufs=PRODUCTS) as chunks,
        tc.psum_pool(name="psum", bufs=PRODUCTS) as psum,
    ):
        offsets = held.tile([ROWS, ENTRIES // GROUP], U16, name="offsets")
        table = held.tile([ROWS, TABLE], F32, name="table")
        weights = held.tile([ROWS, OUTPUTS], BF16, name="weights")
        bias = held.tile([OUTPUTS, 1], F32, name="bias")
        nc.sync.dma_start(offsets[:], offs)
        nc.sync.dma_start(table[:], tab)
        nc.sync.dma_start(weights[:], w)
        nc.sync.dma_start(bias[:], b)

        clamped = []
        for piece in range(PIECES):
            piece_offsets = offsets[:, piece * PIECE // GROUP : (piece + 1) * PIECE // GROUP]
            picked = pieces.tile([ROWS, PIECE], F32, name="picked")
            nc.vector.tensor_scalar(
                picked[:], table[:].indirect(piece_offsets), CLAMP_LOW, CLAMP_HIGH, ALU.max, ALU.min
            )
            clamped += [picked[:, :CHUNK], picked[:, CHUNK:]]

        def multiply(values, round_to_bf16):
            columns = values.shape[1]
            rounded = chunks.tile([ROWS, columns], BF16, name="rounded")
            round_to_bf16(rounded[:], values)
            product = psum.tile([OUTPUTS, columns], F32, name="product")
            nc.tensor.matmul(product[:], weights[:], rounded[:], start=True, stop=True)
            return product

        products = []
        for chunk in range(CHUNKS):
            if chunk < EARLY_CHUNKS:
                products.append([multiply(clamped[chunk], nc.scalar.copy)])
            else:
                products.append([
                    multiply(clamped[chunk][:, :HALF], nc.vector.tensor_copy),
                    multiply(clamped[chunk][:, HALF:], nc.vector.tensor_copy),
                ])

        for chunk in range(CHUNKS):
            result = chunks.tile([OUTPUTS, CHUNK], F32, name="result")
            if chunk < EARLY_CHUNKS:
                nc.scalar.activation(result[:], products[chunk][0][:], ACT.Relu, bias=bias[:])
            else:
                left, right = products[chunk]
                nc.scalar.activation(result[:, :HALF], left[:], ACT.Relu, bias=bias[:])
                nc.vector.tensor_scalar(result[:, HALF:], right[:], bias[:], 0.0, ALU.add, ALU.max)
            nc.sync.dma_start(out[:, chunk * CHUNK : (chunk + 1) * CHUNK], result[:])
